import numpy as np
import ml_dtypes


def mxq(x, axis, fmt="e4m3"):
    dtype, down = {"e4m3": (ml_dtypes.float8_e4m3fn, 7), "e5m2": (ml_dtypes.float8_e5m2, 14)}[fmt]
    v = np.moveaxis(np.asarray(x, np.float32).astype(ml_dtypes.bfloat16).astype(np.float64), axis, -1)
    blocks = v.reshape(v.shape[:-1] + (-1, 32))
    amax = np.abs(blocks).max(-1, keepdims=True)
    byte = np.maximum(np.where(amax > 0, np.frexp(amax)[1] - 1 + 127, 0) - down, 1)
    scale = np.exp2(byte - 127.0)
    codes = (blocks / scale).astype(np.float32).astype(dtype).astype(np.float64)
    return np.moveaxis((codes * scale).reshape(v.shape), -1, axis)


WIDE = False


def mx_kscale(k):
    if not WIDE:
        return np.ones(k)
    levels = np.array([10, -10, 5, -5, 0])
    if k % 512:
        return np.exp2(np.random.permutation(np.resize(levels, k // 32))).repeat(32)
    a = np.empty((k // 512, 16))
    for p in range(k // 512):
        a[p, :8] = np.random.permutation(np.resize(levels, 8))
        for g in range(8):
            far = levels[np.abs(levels - a[p, g]) >= 10]
            a[p, g + 8] = far[np.random.randint(len(far))]
    return np.exp2(a.ravel()).repeat(32)


def f64(x):
    return np.asarray(x).astype(np.float64)


def striped(idx):
    return np.tile(np.asarray(idx).reshape(-1, 16).T, (8, 1)).astype(np.uint16)


def unstriped(offs):
    return offs[:16].T.reshape(-1).astype(np.int64)


E2M1 = np.array([0.0, 0.5, 1.0, 1.5, 2.0, 3.0, 4.0, 6.0, -0.0, -0.5, -1.0, -1.5, -2.0, -3.0, -4.0, -6.0])


def pack_weight(w, fmt):
    k, n = w.shape
    w = f64(np.asarray(w, np.float32).astype(ml_dtypes.bfloat16)).reshape(k // 32, 32, n)
    amax = np.abs(w).max(1)
    if fmt == "e4m3":
        byte = np.frexp(amax)[1] - 1 + 127 - 7
    else:
        mant, ex = np.frexp(amax / 6.0)
        byte = np.where(mant > 0.5, ex, ex - 1) + 127
    byte = np.clip(np.where(amax > 0, byte, 1), 1, 254)
    scaled = (w * np.exp2(127.0 - byte)[:, None, :]).reshape(k, n).astype(np.float32)
    by_word = np.ascontiguousarray(scaled.reshape(k // 512, 128, 4, n).transpose(0, 1, 3, 2))
    if fmt == "e4m3":
        words = by_word.astype(ml_dtypes.float8_e4m3fn).view(np.uint8)
    else:
        c = by_word.astype(ml_dtypes.float4_e2m1fn).view(np.uint8) & 0xF
        words = (c[..., 0::2] | (c[..., 1::2] << 4)).reshape(k // 512, 128, 2 * n)
    return np.ascontiguousarray(words), np.ascontiguousarray(byte.astype(np.uint8).reshape(k // 512, 16, n))


def unpack_weight(words, scales, fmt):
    g, _, n = scales.shape
    words = np.ascontiguousarray(words).reshape(g, 128, n, -1)
    if fmt == "e4m3":
        vals = words.view(ml_dtypes.float8_e4m3fn).astype(np.float64)
    else:
        nib = np.empty((g, 128, n, 4), np.uint8)
        nib[..., 0::2] = words & 0xF
        nib[..., 1::2] = words >> 4
        vals = E2M1[nib]
    vals = vals * np.repeat(np.exp2(scales.astype(np.float64) - 127.0), 8, axis=1)[..., None]
    return vals.transpose(0, 1, 3, 2).reshape(g * 512, n)


def sigmoid(v):
    return 1.0 / (1.0 + np.exp(-v))


def bf(x):
    return np.asarray(x, np.float32).astype(ml_dtypes.bfloat16)


def planes(Y):
    r, m = Y.shape
    b = f64(bf(Y)).reshape(r // 32, 32, m)
    amax = np.abs(b).max(1)
    byte = np.clip(np.where(amax > 0, np.frexp(amax)[1] - 1 + 127 - 7, 1), 1, 254)
    codes = (b * np.exp2(127.0 - byte)[:, None, :]).reshape(r, m).astype(np.float32).astype(ml_dtypes.float8_e4m3fn).view(np.uint8)
    words = codes.reshape(r // 512, 128, 4, m).transpose(0, 1, 3, 2)
    return np.ascontiguousarray(words), np.ascontiguousarray(byte.astype(np.uint8).reshape(r // 512, 16, m))


D, E, T, I, Q = 512, 512, 2048, 512, 256


def setup_inputs():
    n = np.random.standard_normal
    idx = np.random.permutation(T)[:I]
    fd = mx_kscale(D)
    fi = mx_kscale(I)
    ti = np.ones(T)
    ti[idx] = fi
    keysp = pack_weight(n((D, T)) / fd[:, None], "e2m1")
    return {
        "query": (n((D, Q)) * 1.0 / np.sqrt(D) * fd[:, None]).astype(np.float32),
        "dquery": (n((D, Q)) * 1.0 / np.sqrt(D) * fd[:, None]).astype(np.float32),
        "query2": (n((D, Q)) * 1.0 / np.sqrt(D) * fd[:, None]).astype(np.float32),
        "keys_words": keysp[0],
        "keys_scales": keysp[1],
        "th": (np.random.uniform(0.3, 1.5, (Q, 1))).astype(np.float32),
        "os": (np.random.uniform(4.0, 16.0, (1, I)) * fi).astype(np.float32),
        "vals": (n((E, T)) / ti).astype(np.float32),
        "offs": striped(idx),
    }


def reference(query, dquery, query2, keys_words, keys_scales, th, os, vals, offs):
    idx = unstriped(offs)
    keysu = unpack_weight(keys_words, keys_scales, "e2m1")
    queryq = mxq(f64(query), 0, "e4m3")
    keysidxg = keysu[:, idx]
    a = queryq.T @ keysidxg
    dqueryq = mxq(f64(dquery), 0, "e4m3")
    ta = dqueryq.T @ keysidxg
    query2q = mxq(f64(query2), 0, "e4m3")
    b = query2q.T @ keysidxg
    ua = sigmoid(a - f64(th))
    ub = sigmoid(b - f64(th))
    p = 1.0 - (1.0 - ua) * (1.0 - ub)
    tua = ta * ua * (1.0 - ua)
    tp = tua * (-1.0) * (1.0 - ub) * (-1.0)
    tw = (tp - np.sum(tp, axis=1, keepdims=True) * p / np.sum(p, axis=1, keepdims=True)) / np.sum(p, axis=1, keepdims=True)
    wo1 = tw * f64(os)
    wt1 = wo1.T
    vt1 = f64(vals)[:, idx].T
    vt1q = mxq(vt1, 0, "e4m3")
    wt1q = mxq(wt1, 0, "e4m3")
    o = vt1q.T @ wt1q
    words, scales = planes(o)
    return o, words, scales

@@ -1,0 +1,184 @@
+from contextlib import ExitStack
+
+import concourse.mybir as mybir
+from concourse.masks import make_identity
+
+D, E, T, I, Q = 512, 512, 2048, 512, 256
+P = 128
+PACK = 4
+HALVES = Q // P
+FLOPS = 2 * (3 * D * Q * I + I * E * Q)
+
+F32 = mybir.dt.float32
+BF16 = mybir.dt.bfloat16
+I32 = mybir.dt.int32
+U32 = mybir.dt.uint32
+U16 = mybir.dt.uint16
+U8 = mybir.dt.uint8
+FP8X4 = mybir.dt.float8_e4m3fn_x4
+FP4X4 = mybir.dt.float4_e2m1fn_x4
+ALU = mybir.AluOpType
+ACT = mybir.ActivationFunctionType
+
+
+def tile_attend_tteitherquestion_pl_kernel(
+    tc, query, dquery, query2, keys_words, keys_scales, th, slot_factor, vals, offs, out_0, out_1, out_2
+):
+    nc = tc.nc
+    with ExitStack() as ctx:
+        sb = ctx.enter_context(tc.tile_pool(name="sb", bufs=1))
+        psum = ctx.enter_context(tc.psum_pool(name="psum", bufs=1))
+
+        def tile(shape, dtype, name):
+            return sb.tile(shape, dtype, name=name, align_bytes=64)
+
+        def bank(shape, tag):
+            return psum.tile(shape, F32, name=tag, tag=tag)
+
+        offsets = sb.tile([P, I // 16], U16, name="offsets")
+        nc.sync.dma_start(offsets[:], offs)
+        key_scales = tile([P, T], U8, "key_scales")
+        nc.vector.memset(key_scales[:].bitcast(I32), 0)
+        key_words = tile([P, T], U16, "key_words")
+        nc.sync.dma_start(key_words[:].bitcast(I32), keys_words[0].bitcast(I32))
+        for g in range(4):
+            nc.sync.dma_start(
+                key_scales[32 * g : 32 * g + 4, :].bitcast(I32),
+                keys_scales[0, 4 * g : 4 * g + 4, :].bitcast(I32),
+            )
+        raw = {}
+        th_pos = tile([P, HALVES], F32, "th_pos")
+        os_sb = tile([P, PACK], F32, "os_sb")
+        for name, src in (("a", query), ("b", query2), ("ta", dquery)):
+            raw[name] = tile([P, PACK, Q], F32, "raw_" + name)
+            nc.sync.dma_start(raw[name][:], src.rearrange("(p t) q -> p t q", t=PACK))
+            if name == "b":
+                with nc.allow_non_contiguous_dma(reason="one threshold to a partition"):
+                    nc.sync.dma_start(th_pos[:], th.rearrange("(h p) o -> p (h o)", p=P))
+        val_planes = vals.rearrange("(p t) n -> t p n", t=PACK)
+        pools = []
+        for t in range(PACK):
+            pools.append(tile([P, T], F32, "vals_%d" % t))
+            nc.sync.dma_start(pools[t][:], val_planes[t])
+            if t == 0:
+                nc.sync.dma_start(os_sb[:], slot_factor.rearrange("o (s r) -> (o s) r", r=PACK))
+
+        ident = tile([P, P], F32, "ident")
+        make_identity(nc, ident[:])
+        warm = tile([P, 1], F32, "warm")
+        nc.scalar.activation(warm[:], ident[:, 0:1], ACT.Sigmoid)
+        th_neg = tile([P, HALVES], F32, "th_neg")
+        nc.scalar.activation(th_neg[:], th_pos[:], ACT.Copy, scale=-1.0)
+
+        kw = tile([P, I], U16, "kw")
+        nc.vector.tensor_copy(kw[:], key_words[:].indirect(offsets[:]))
+        ks = tile([P, I], U8, "ks")
+        nc.vector.tensor_copy(ks[:], key_scales[:].indirect(offsets[:]))
+
+        q_codes, q_scales = {}, {}
+        for name, copy in (("a", nc.scalar.copy), ("b", nc.scalar.copy), ("ta", nc.vector.tensor_copy)):
+            grouped = tile([P, Q * PACK], BF16, "grouped_" + name)
+            copy(
+                grouped[:].rearrange("p (c i t) -> p c t i", i=4, t=PACK),
+                raw[name][:].rearrange("p t (c i) -> p c t i", i=4),
+            )
+            q_codes[name] = tile([P, Q], U32, "codes_" + name)
+            q_scales[name] = tile([P, Q], U8, "scales_" + name)
+            nc.vector.quantize_mx(q_codes[name][:].bitcast(FP8X4), q_scales[name][:], grouped[:])
+
+        scores = {}
+        for name in ("a", "b", "ta"):
+            for h in range(HALVES):
+                cols = slice(h * P, (h + 1) * P)
+                scores[name, h] = bank([P, I], "%s%d" % (name, h))
+                nc.tensor.matmul_mx(
+                    scores[name, h][:],
+                    lhsT=q_codes[name][:, cols].bitcast(FP8X4),
+                    lhsT_scale=q_scales[name][:, cols],
+                    rhs=kw[:].bitcast(FP4X4),
+                    rhs_scale=ks[:],
+                    start=True,
+                    stop=True,
+                )
+
+        def dealt(ap):
+            return ap.rearrange("q (s r) -> q r s", r=PACK)
+
+        w_codes, w_scales = [], []
+        for h in range(HALVES):
+            def wide(name):
+                return tile([P, PACK, P], F32, "%s_%d" % (name, h))
+
+            def column(name):
+                return tile([P, 1], F32, "%s_%d" % (name, h))
+
+            ua, nb, m_neg, p_neg, x, tp, kp = [wide(n) for n in ("ua", "nb", "m_neg", "p_neg", "x", "tp", "kp")]
+            sum_neg, r_neg, c, k = [column(n) for n in ("sum_neg", "r_neg", "c", "k")]
+            nc.scalar.activation(ua[:], dealt(scores["a", h][:]), ACT.Sigmoid, bias=th_neg[:, h : h + 1])
+            nc.scalar.activation(nb[:], dealt(scores["b", h][:]), ACT.Sigmoid, bias=th_pos[:, h : h + 1], scale=-1.0)
+            nc.vector.scalar_tensor_tensor(m_neg[:], ua[:], 1.0, nb[:], ALU.subtract, ALU.mult)
+            nc.scalar.activation(p_neg[:], m_neg[:], ACT.Identity, bias=-1.0, scale=-1.0, accum_out=sum_neg[:])
+            nc.vector.tensor_tensor(x[:], dealt(scores["ta", h][:]), ua[:], ALU.mult)
+            nc.vector.reciprocal(r_neg[:], sum_neg[:])
+            nc.vector.scalar_tensor_tensor(tp[:], x[:], r_neg[:], m_neg[:], ALU.mult, ALU.mult, accum_out=c[:])
+            nc.scalar.activation(k[:], c[:], ACT.Copy, scale=r_neg[:])
+            nc.scalar.activation(kp[:], m_neg[:], ACT.Identity, bias=k[:], scale=k[:])
+            turned = bank([P, PACK, P], "a%d" % h)
+            for j, term in enumerate((tp, kp)):
+                for r in range(PACK):
+                    nc.tensor.matmul(
+                        turned[:, r, :], term[:, r, :], ident[:], is_transpose=True,
+                        start=(j == 0 and r == 0), stop=(j == 1 and r == PACK - 1),
+                    )
+            w = tile([P, P, PACK], BF16, "w_%d" % h)
+            nc.vector.tensor_tensor(
+                w[:], turned[:].rearrange("s r q -> s q r"),
+                os_sb[:].unsqueeze(1).to_broadcast([P, P, PACK]), ALU.mult,
+            )
+            w_codes.append(tile([P, P], U32, "w_codes_%d" % h))
+            w_scales.append(tile([P, P], U8, "w_scales_%d" % h))
+            nc.vector.quantize_mx(w_codes[h][:].bitcast(FP8X4), w_scales[h][:], w[:].rearrange("s q r -> s (q r)"))
+
+        acc = [bank([P, PACK, P], "b%d" % h) for h in range(HALVES)]
+        result = tile([P, PACK, Q], F32, "result")
+        out_rows = out_0.rearrange("(p t) q -> p t q", t=PACK)
+        for t in range(PACK):
+            picked = tile([P, I], BF16, "picked_%d" % t)
+            nc.vector.tensor_copy(picked[:], pools[t][:].indirect(offsets[:]))
+            pairs = picked[:].bitcast(F32)
+            vt = bank([P, 2, P], "vt%d" % (t % 2))
+            for u in range(2):
+                nc.tensor.transpose(vt[:, u, :], pairs[:, u : I // 2 : 2], ident[:])
+            v = tile([P, P * PACK], BF16, "v_%d" % t)
+            nc.scalar.copy(v[:].bitcast(F32).rearrange("s (c u) -> s c u", u=2), vt[:].rearrange("s u c -> s c u"))
+            v_codes = tile([P, P], U32, "v_codes_%d" % t)
+            v_scales = tile([P, P], U8, "v_scales_%d" % t)
+            nc.vector.quantize_mx(v_codes[:].bitcast(FP8X4), v_scales[:], v[:])
+            for h in range(HALVES):
+                nc.tensor.matmul_mx(
+                    acc[h][:, t, :],
+                    lhsT=v_codes[:].bitcast(FP8X4), lhsT_scale=v_scales[:],
+                    rhs=w_codes[h][:].bitcast(FP8X4), rhs_scale=w_scales[h][:],
+                    start=True, stop=True,
+                )
+            if t == PACK - 2:
+                for h in range(HALVES):
+                    nc.scalar.copy(result[:, : PACK - 1, h * P : (h + 1) * P], acc[h][:, : PACK - 1, :])
+                nc.sync.dma_start(out_rows[:, : PACK - 1, :], result[:, : PACK - 1, :])
+
+        o_grouped = tile([P, Q, PACK], BF16, "o_grouped")
+        for h, copy in enumerate((nc.vector.tensor_copy, nc.scalar.copy)):
+            copy(o_grouped[:, h * P : (h + 1) * P, :], acc[h][:].rearrange("p t q -> p q t"))
+        for h in range(HALVES):
+            nc.scalar.copy(result[:, PACK - 1, h * P : (h + 1) * P], acc[h][:, PACK - 1, :])
+        nc.scalar.dma_start(out_rows[:, PACK - 1, :], result[:, PACK - 1, :])
+        o_codes = tile([P, Q], U32, "o_codes")
+        o_scales = tile([P, Q], U8, "o_scales")
+        nc.vector.quantize_mx(o_codes[:].bitcast(FP8X4), o_scales[:], o_grouped[:].rearrange("p q t -> p (q t)"))
+        nc.sync.dma_start(out_1[0].rearrange("p c t -> p (c t)").bitcast(I32), o_codes[:].bitcast(I32))
+        for g in range(4):
+            queue = nc.sync if g % 2 == 0 else nc.scalar
+            queue.dma_start(
+                out_2[0, 4 * g : 4 * g + 4, :].bitcast(I32),
+                o_scales[32 * g : 32 * g + 4, :].bitcast(I32),
+            )

@@ -7,6 +7,7 @@ D, E, T, I, Q = 512, 512, 2048, 512, 256
 P = 128
 PACK = 4
 HALVES = Q // P
+CAST_PIECE = 512
 FLOPS = 2 * (3 * D * Q * I + I * E * Q)
 
 F32 = mybir.dt.float32
@@ -29,8 +30,8 @@ def tile_attend_tteitherquestion_pl_kernel(
         sb = ctx.enter_context(tc.tile_pool(name="sb", bufs=1))
         psum = ctx.enter_context(tc.psum_pool(name="psum", bufs=1))
 
-        def tile(shape, dtype, name):
-            return sb.tile(shape, dtype, name=name, align_bytes=64)
+        def tile(shape, dtype, name, tag=None):
+            return sb.tile(shape, dtype, name=name, tag=tag or name, align_bytes=64)
 
         def bank(shape, tag):
             return psum.tile(shape, F32, name=tag, tag=tag)
@@ -38,21 +39,20 @@ def tile_attend_tteitherquestion_pl_kernel(
         offsets = sb.tile([P, I // 16], U16, name="offsets")
         nc.sync.dma_start(offsets[:], offs)
         key_scales = tile([P, T], U8, "key_scales")
-        nc.vector.memset(key_scales[:].bitcast(I32), 0)
-        key_words = tile([P, T], U16, "key_words")
-        nc.sync.dma_start(key_words[:].bitcast(I32), keys_words[0].bitcast(I32))
         for g in range(4):
             nc.sync.dma_start(
-                key_scales[32 * g : 32 * g + 4, :].bitcast(I32),
-                keys_scales[0, 4 * g : 4 * g + 4, :].bitcast(I32),
+                key_scales[32 * g : 32 * (g + 1), :].bitcast(I32),
+                keys_scales[0, 4 * g : 4 * g + 4, :].bitcast(I32).partition_broadcast(8),
             )
+        key_words = tile([P, T], U16, "key_words")
+        nc.sync.dma_start(key_words[:].bitcast(I32), keys_words[0].bitcast(I32))
         raw = {}
         th_pos = tile([P, HALVES], F32, "th_pos")
         os_sb = tile([P, PACK], F32, "os_sb")
         for name, src in (("a", query), ("b", query2), ("ta", dquery)):
             raw[name] = tile([P, PACK, Q], F32, "raw_" + name)
             nc.sync.dma_start(raw[name][:], src.rearrange("(p t) q -> p t q", t=PACK))
-            if name == "b":
+            if name == "a":
                 with nc.allow_non_contiguous_dma(reason="one threshold to a partition"):
                     nc.sync.dma_start(th_pos[:], th.rearrange("(h p) o -> p (h o)", p=P))
         val_planes = vals.rearrange("(p t) n -> t p n", t=PACK)
@@ -68,33 +68,31 @@ def tile_attend_tteitherquestion_pl_kernel(
         warm = tile([P, 1], F32, "warm")
         nc.scalar.activation(warm[:], ident[:, 0:1], ACT.Sigmoid)
         th_neg = tile([P, HALVES], F32, "th_neg")
-        nc.scalar.activation(th_neg[:], th_pos[:], ACT.Copy, scale=-1.0)
+        nc.gpsimd.tensor_scalar(th_neg[:], th_pos[:], -1.0, 0.0, ALU.mult, ALU.add)
 
-        kw = tile([P, I], U16, "kw")
-        nc.vector.tensor_copy(kw[:], key_words[:].indirect(offsets[:]))
         ks = tile([P, I], U8, "ks")
         nc.vector.tensor_copy(ks[:], key_scales[:].indirect(offsets[:]))
-
-        q_codes, q_scales = {}, {}
-        for name, copy in (("a", nc.scalar.copy), ("b", nc.scalar.copy), ("ta", nc.vector.tensor_copy)):
-            grouped = tile([P, Q * PACK], BF16, "grouped_" + name)
-            copy(
-                grouped[:].rearrange("p (c i t) -> p c t i", i=4, t=PACK),
-                raw[name][:].rearrange("p t (c i) -> p c t i", i=4),
-            )
-            q_codes[name] = tile([P, Q], U32, "codes_" + name)
-            q_scales[name] = tile([P, Q], U8, "scales_" + name)
-            nc.vector.quantize_mx(q_codes[name][:].bitcast(FP8X4), q_scales[name][:], grouped[:])
+        kw = tile([P, I], U16, "kw")
+        nc.vector.tensor_copy(kw[:], key_words[:].indirect(offsets[:]))
 
         scores = {}
         for name in ("a", "b", "ta"):
+            grouped = []
             for h in range(HALVES):
-                cols = slice(h * P, (h + 1) * P)
+                grouped.append(tile([P, P * PACK], BF16, "grouped_%s%d" % (name, h)))
+                nc.vector.tensor_copy(
+                    grouped[h][:].rearrange("p (c i t) -> p c t i", i=4, t=PACK),
+                    raw[name][:, :, h * P : (h + 1) * P].rearrange("p t (c i) -> p c t i", i=4),
+                )
+            for h in range(HALVES):
+                codes = tile([P, P], U32, "codes_%s%d" % (name, h))
+                scales = tile([P, P], U8, "scales_%s%d" % (name, h))
+                nc.vector.quantize_mx(codes[:].bitcast(FP8X4), scales[:], grouped[h][:])
                 scores[name, h] = bank([P, I], "%s%d" % (name, h))
                 nc.tensor.matmul_mx(
                     scores[name, h][:],
-                    lhsT=q_codes[name][:, cols].bitcast(FP8X4),
-                    lhsT_scale=q_scales[name][:, cols],
+                    lhsT=codes[:].bitcast(FP8X4),
+                    lhsT_scale=scales[:],
                     rhs=kw[:].bitcast(FP4X4),
                     rhs_scale=ks[:],
                     start=True,
@@ -105,6 +103,7 @@ def tile_attend_tteitherquestion_pl_kernel(
             return ap.rearrange("q (s r) -> q r s", r=PACK)
 
         w_codes, w_scales = [], []
+        terms = []
         for h in range(HALVES):
             def wide(name):
                 return tile([P, PACK, P], F32, "%s_%d" % (name, h))
@@ -123,62 +122,76 @@ def tile_attend_tteitherquestion_pl_kernel(
             nc.vector.scalar_tensor_tensor(tp[:], x[:], r_neg[:], m_neg[:], ALU.mult, ALU.mult, accum_out=c[:])
             nc.scalar.activation(k[:], c[:], ACT.Copy, scale=r_neg[:])
             nc.scalar.activation(kp[:], m_neg[:], ACT.Identity, bias=k[:], scale=k[:])
-            turned = bank([P, PACK, P], "a%d" % h)
-            for j, term in enumerate((tp, kp)):
-                for r in range(PACK):
-                    nc.tensor.matmul(
-                        turned[:, r, :], term[:, r, :], ident[:], is_transpose=True,
-                        start=(j == 0 and r == 0), stop=(j == 1 and r == PACK - 1),
-                    )
-            w = tile([P, P, PACK], BF16, "w_%d" % h)
-            nc.vector.tensor_tensor(
-                w[:], turned[:].rearrange("s r q -> s q r"),
-                os_sb[:].unsqueeze(1).to_broadcast([P, P, PACK]), ALU.mult,
-            )
-            w_codes.append(tile([P, P], U32, "w_codes_%d" % h))
-            w_scales.append(tile([P, P], U8, "w_scales_%d" % h))
-            nc.vector.quantize_mx(w_codes[h][:].bitcast(FP8X4), w_scales[h][:], w[:].rearrange("s q r -> s (q r)"))
+            terms.append((tp, kp))
 
-        acc = [bank([P, PACK, P], "b%d" % h) for h in range(HALVES)]
-        result = tile([P, PACK, Q], F32, "result")
-        out_rows = out_0.rearrange("(p t) q -> p t q", t=PACK)
-        for t in range(PACK):
-            picked = tile([P, I], BF16, "picked_%d" % t)
-            nc.vector.tensor_copy(picked[:], pools[t][:].indirect(offsets[:]))
+        v_codes, v_scales = {}, {}
+
+        def turn_values(t, picked):
             pairs = picked[:].bitcast(F32)
             vt = bank([P, 2, P], "vt%d" % (t % 2))
             for u in range(2):
                 nc.tensor.transpose(vt[:, u, :], pairs[:, u : I // 2 : 2], ident[:])
             v = tile([P, P * PACK], BF16, "v_%d" % t)
             nc.scalar.copy(v[:].bitcast(F32).rearrange("s (c u) -> s c u", u=2), vt[:].rearrange("s u c -> s c u"))
-            v_codes = tile([P, P], U32, "v_codes_%d" % t)
-            v_scales = tile([P, P], U8, "v_scales_%d" % t)
-            nc.vector.quantize_mx(v_codes[:].bitcast(FP8X4), v_scales[:], v[:])
-            for h in range(HALVES):
+            v_codes[t] = tile([P, P], U32, "v_codes_%d" % t)
+            v_scales[t] = tile([P, P], U8, "v_scales_%d" % t)
+            nc.vector.quantize_mx(v_codes[t][:].bitcast(FP8X4), v_scales[t][:], v[:])
+
+        pool_bf16 = tile([P, T], BF16, "pool_bf16", "th_pos")
+        for c0 in range(0, T, CAST_PIECE):
+            nc.scalar.activation(pool_bf16[:, c0 : c0 + CAST_PIECE], pools[0][:, c0 : c0 + CAST_PIECE], ACT.Copy)
+        picked = tile([P, I], BF16, "picked_0")
+        nc.scalar.activation(picked[:], pool_bf16[:].indirect(offsets[:]), ACT.Copy)
+        turn_values(0, picked)
+
+        for t in range(1, PACK):
+            picked = tile([P, I], BF16, "picked_%d" % t, {1: "ua_1", 2: "x_1"}.get(t))
+            nc.vector.tensor_copy(picked[:], pools[t][:].indirect(offsets[:]))
+            turn_values(t, picked)
+
+        w_both = tile([P, HALVES, P, PACK], BF16, "w_both", "vals_3")
+        for h in range(HALVES):
+            turned = bank([P, PACK, P], "a%d" % h)
+            for j, term in enumerate(terms[h]):
+                for r in range(PACK):
+                    nc.tensor.matmul(
+                        turned[:, r, :], term[:, r, :], ident[:], is_transpose=True,
+                        start=(j == 0 and r == 0), stop=(j == 1 and r == PACK - 1),
+                    )
+            w = w_both[:, h]
+            nc.vector.tensor_tensor(
+                w, turned[:].rearrange("s r q -> s q r"),
+                os_sb[:].unsqueeze(1).to_broadcast([P, P, PACK]), ALU.mult,
+            )
+            w_codes.append(tile([P, P], U32, "w_codes_%d" % h))
+            w_scales.append(tile([P, P], U8, "w_scales_%d" % h))
+            nc.vector.quantize_mx(w_codes[h][:].bitcast(FP8X4), w_scales[h][:], w.rearrange("s q r -> s (q r)"))
+
+        out_rows = out_0.rearrange("(p t) (h q) -> h p t q", t=PACK, h=HALVES)
+        out_words = out_1[0].rearrange("p c t -> p (c t)").bitcast(I32)
+        o_codes = tile([P, Q], U32, "o_codes")
+        o_scales = tile([P, Q], U8, "o_scales")
+        for h, copy in enumerate((nc.scalar.copy, nc.vector.tensor_copy)):
+            cols = slice(h * P, (h + 1) * P)
+            acc = bank([P, PACK, P], "b%d" % h)
+            for t in range(PACK):
                 nc.tensor.matmul_mx(
-                    acc[h][:, t, :],
-                    lhsT=v_codes[:].bitcast(FP8X4), lhsT_scale=v_scales[:],
+                    acc[:, t, :],
+                    lhsT=v_codes[t][:].bitcast(FP8X4), lhsT_scale=v_scales[t][:],
                     rhs=w_codes[h][:].bitcast(FP8X4), rhs_scale=w_scales[h][:],
                     start=True, stop=True,
                 )
-            if t == PACK - 2:
-                for h in range(HALVES):
-                    nc.scalar.copy(result[:, : PACK - 1, h * P : (h + 1) * P], acc[h][:, : PACK - 1, :])
-                nc.sync.dma_start(out_rows[:, : PACK - 1, :], result[:, : PACK - 1, :])
-
-        o_grouped = tile([P, Q, PACK], BF16, "o_grouped")
-        for h, copy in enumerate((nc.vector.tensor_copy, nc.scalar.copy)):
-            copy(o_grouped[:, h * P : (h + 1) * P, :], acc[h][:].rearrange("p t q -> p q t"))
-        for h in range(HALVES):
-            nc.scalar.copy(result[:, PACK - 1, h * P : (h + 1) * P], acc[h][:, PACK - 1, :])
-        nc.scalar.dma_start(out_rows[:, PACK - 1, :], result[:, PACK - 1, :])
-        o_codes = tile([P, Q], U32, "o_codes")
-        o_scales = tile([P, Q], U8, "o_scales")
-        nc.vector.quantize_mx(o_codes[:].bitcast(FP8X4), o_scales[:], o_grouped[:].rearrange("p q t -> p (q t)"))
-        nc.sync.dma_start(out_1[0].rearrange("p c t -> p (c t)").bitcast(I32), o_codes[:].bitcast(I32))
+            o_grouped = tile([P, P, PACK], BF16, "o_grouped_%d" % h)
+            copy(o_grouped[:], acc[:].rearrange("p t q -> p q t"))
+            result = tile([P, PACK, P], F32, "result_%d" % h)
+            nc.scalar.copy(result[:], acc[:])
+            nc.scalar.dma_start(out_rows[h], result[:])
+            nc.vector.quantize_mx(
+                o_codes[:, cols].bitcast(FP8X4), o_scales[:, cols], o_grouped[:].rearrange("p q t -> p (q t)")
+            )
+            nc.sync.dma_start(out_words[:, cols], o_codes[:, cols].bitcast(I32))
         for g in range(4):
-            queue = nc.sync if g % 2 == 0 else nc.scalar
-            queue.dma_start(
+            nc.sync.dma_start(
                 out_2[0, 4 * g : 4 * g + 4, :].bitcast(I32),
                 o_scales[32 * g : 32 * g + 4, :].bitcast(I32),
             )

@@ -7,7 +7,11 @@ D, E, T, I, Q = 512, 512, 2048, 512, 256
 P = 128
 PACK = 4
 HALVES = Q // P
+QUADRANT = 32
+RUN = 4
 CAST_PIECE = 512
+SCALAR_PLANE = 0
+LAST_PLANE = PACK - 1
 FLOPS = 2 * (3 * D * Q * I + I * E * Q)
 
 F32 = mybir.dt.float32
@@ -28,10 +32,14 @@ def tile_attend_tteitherquestion_pl_kernel(
     nc = tc.nc
     with ExitStack() as ctx:
         sb = ctx.enter_context(tc.tile_pool(name="sb", bufs=1))
+        late = ctx.enter_context(tc.tile_pool(name="late", bufs=1))
         psum = ctx.enter_context(tc.psum_pool(name="psum", bufs=1))
 
-        def tile(shape, dtype, name, tag=None):
-            return sb.tile(shape, dtype, name=name, tag=tag or name, align_bytes=64)
+        def tile(shape, dtype, name, reuse=None):
+            return sb.tile(shape, dtype, name=name, tag=reuse or name, align_bytes=64)
+
+        def late_tile(shape, dtype, name, offset):
+            return late.tile(shape, dtype, name=name, align_bytes=64, offset=offset)
 
         def bank(shape, tag):
             return psum.tile(shape, F32, name=tag, tag=tag)
@@ -39,29 +47,27 @@ def tile_attend_tteitherquestion_pl_kernel(
         offsets = sb.tile([P, I // 16], U16, name="offsets")
         nc.sync.dma_start(offsets[:], offs)
         key_scales = tile([P, T], U8, "key_scales")
-        for g in range(4):
+        for g in range(P // QUADRANT):
             nc.sync.dma_start(
-                key_scales[32 * g : 32 * (g + 1), :].bitcast(I32),
-                keys_scales[0, 4 * g : 4 * g + 4, :].bitcast(I32).partition_broadcast(8),
+                key_scales[QUADRANT * g : QUADRANT * (g + 1), :].bitcast(I32),
+                keys_scales[0, 4 * g : 4 * g + 4, :].bitcast(I32).partition_broadcast(QUADRANT // 4),
             )
         key_words = tile([P, T], U16, "key_words")
         nc.sync.dma_start(key_words[:].bitcast(I32), keys_words[0].bitcast(I32))
         raw = {}
         th_pos = tile([P, HALVES], F32, "th_pos")
-        os_sb = tile([P, PACK], F32, "os_sb")
+        factor = tile([P, PACK], F32, "factor")
         for name, src in (("a", query), ("b", query2), ("ta", dquery)):
             raw[name] = tile([P, PACK, Q], F32, "raw_" + name)
             nc.sync.dma_start(raw[name][:], src.rearrange("(p t) q -> p t q", t=PACK))
-            if name == "a":
-                with nc.allow_non_contiguous_dma(reason="one threshold to a partition"):
-                    nc.sync.dma_start(th_pos[:], th.rearrange("(h p) o -> p (h o)", p=P))
+        with nc.allow_non_contiguous_dma(reason="one threshold to a partition for each half of the rows"):
+            nc.scalar.dma_start(th_pos[:], th.rearrange("(h p) o -> p (h o)", p=P))
+        nc.scalar.dma_start(factor[:], slot_factor.rearrange("o (s r) -> (o s) r", r=PACK))
         val_planes = vals.rearrange("(p t) n -> t p n", t=PACK)
         pools = []
         for t in range(PACK):
-            pools.append(tile([P, T], F32, "vals_%d" % t))
+            pools.append(late_tile([P, T], F32, "vals_last", 0) if t == LAST_PLANE else tile([P, T], F32, "vals_%d" % t))
             nc.sync.dma_start(pools[t][:], val_planes[t])
-            if t == 0:
-                nc.sync.dma_start(os_sb[:], slot_factor.rearrange("o (s r) -> (o s) r", r=PACK))
 
         ident = tile([P, P], F32, "ident")
         make_identity(nc, ident[:])
@@ -70,10 +76,10 @@ def tile_attend_tteitherquestion_pl_kernel(
         th_neg = tile([P, HALVES], F32, "th_neg")
         nc.gpsimd.tensor_scalar(th_neg[:], th_pos[:], -1.0, 0.0, ALU.mult, ALU.add)
 
-        ks = tile([P, I], U8, "ks")
-        nc.vector.tensor_copy(ks[:], key_scales[:].indirect(offsets[:]))
-        kw = tile([P, I], U16, "kw")
-        nc.vector.tensor_copy(kw[:], key_words[:].indirect(offsets[:]))
+        picked_scales = tile([P, I], U8, "picked_scales")
+        nc.vector.tensor_copy(picked_scales[:], key_scales[:].indirect(offsets[:]))
+        picked_words = tile([P, I], U16, "picked_words")
+        nc.vector.tensor_copy(picked_words[:], key_words[:].indirect(offsets[:]))
 
         scores = {}
         for name in ("a", "b", "ta"):
@@ -81,8 +87,8 @@ def tile_attend_tteitherquestion_pl_kernel(
             for h in range(HALVES):
                 grouped.append(tile([P, P * PACK], BF16, "grouped_%s%d" % (name, h)))
                 nc.vector.tensor_copy(
-                    grouped[h][:].rearrange("p (c i t) -> p c t i", i=4, t=PACK),
-                    raw[name][:, :, h * P : (h + 1) * P].rearrange("p t (c i) -> p c t i", i=4),
+                    grouped[h][:].rearrange("p (c i t) -> p c t i", i=RUN, t=PACK),
+                    raw[name][:, :, h * P : (h + 1) * P].rearrange("p t (c i) -> p c t i", i=RUN),
                 )
             for h in range(HALVES):
                 codes = tile([P, P], U32, "codes_%s%d" % (name, h))
@@ -93,105 +99,122 @@ def tile_attend_tteitherquestion_pl_kernel(
                     scores[name, h][:],
                     lhsT=codes[:].bitcast(FP8X4),
                     lhsT_scale=scales[:],
-                    rhs=kw[:].bitcast(FP4X4),
-                    rhs_scale=ks[:],
+                    rhs=picked_words[:].bitcast(FP4X4),
+                    rhs_scale=picked_scales[:],
                     start=True,
                     stop=True,
                 )
 
-        def dealt(ap):
-            return ap.rearrange("q (s r) -> q r s", r=PACK)
-
-        w_codes, w_scales = [], []
         terms = []
         for h in range(HALVES):
-            def wide(name):
-                return tile([P, PACK, P], F32, "%s_%d" % (name, h))
-
-            def column(name):
-                return tile([P, 1], F32, "%s_%d" % (name, h))
-
-            ua, nb, m_neg, p_neg, x, tp, kp = [wide(n) for n in ("ua", "nb", "m_neg", "p_neg", "x", "tp", "kp")]
-            sum_neg, r_neg, c, k = [column(n) for n in ("sum_neg", "r_neg", "c", "k")]
-            nc.scalar.activation(ua[:], dealt(scores["a", h][:]), ACT.Sigmoid, bias=th_neg[:, h : h + 1])
-            nc.scalar.activation(nb[:], dealt(scores["b", h][:]), ACT.Sigmoid, bias=th_pos[:, h : h + 1], scale=-1.0)
+            ua, nb, m_neg, p_neg, x, tp_term, p_term = [
+                tile([P, I], F32, "%s_%d" % (name, h))
+                for name in ("ua", "nb", "m_neg", "p_neg", "x", "tp_term", "p_term")
+            ]
+            sum_neg, r_neg, c, k = [tile([P, 1], F32, "%s_%d" % (name, h)) for name in ("sum_neg", "r_neg", "c", "k")]
+            nc.scalar.activation(ua[:], scores["a", h][:], ACT.Sigmoid, bias=th_neg[:, h : h + 1])
+            nc.scalar.activation(nb[:], scores["b", h][:], ACT.Sigmoid, bias=th_pos[:, h : h + 1], scale=-1.0)
             nc.vector.scalar_tensor_tensor(m_neg[:], ua[:], 1.0, nb[:], ALU.subtract, ALU.mult)
             nc.scalar.activation(p_neg[:], m_neg[:], ACT.Identity, bias=-1.0, scale=-1.0, accum_out=sum_neg[:])
-            nc.vector.tensor_tensor(x[:], dealt(scores["ta", h][:]), ua[:], ALU.mult)
+            nc.vector.tensor_tensor(x[:], scores["ta", h][:], ua[:], ALU.mult)
             nc.vector.reciprocal(r_neg[:], sum_neg[:])
-            nc.vector.scalar_tensor_tensor(tp[:], x[:], r_neg[:], m_neg[:], ALU.mult, ALU.mult, accum_out=c[:])
+            nc.vector.scalar_tensor_tensor(tp_term[:], x[:], r_neg[:], m_neg[:], ALU.mult, ALU.mult, accum_out=c[:])
             nc.scalar.activation(k[:], c[:], ACT.Copy, scale=r_neg[:])
-            nc.scalar.activation(kp[:], m_neg[:], ACT.Identity, bias=k[:], scale=k[:])
-            terms.append((tp, kp))
+            nc.scalar.activation(
+                p_term[:].rearrange("q (r s) -> q s r", r=PACK),
+                m_neg[:].rearrange("q (s r) -> q s r", r=PACK),
+                ACT.Identity,
+                bias=k[:],
+                scale=k[:],
+            )
+            terms.append(
+                (tp_term[:].rearrange("q (s r) -> q r s", r=PACK), p_term[:].rearrange("q (r s) -> q r s", r=PACK))
+            )
 
-        v_codes, v_scales = {}, {}
+        v_turned = {}
 
-        def turn_values(t, picked):
+        def turn_values(t, picked, tag):
             pairs = picked[:].bitcast(F32)
-            vt = bank([P, 2, P], "vt%d" % (t % 2))
+            turned_pairs = bank([P, 2, P], tag)
             for u in range(2):
-                nc.tensor.transpose(vt[:, u, :], pairs[:, u : I // 2 : 2], ident[:])
-            v = tile([P, P * PACK], BF16, "v_%d" % t)
-            nc.scalar.copy(v[:].bitcast(F32).rearrange("s (c u) -> s c u", u=2), vt[:].rearrange("s u c -> s c u"))
-            v_codes[t] = tile([P, P], U32, "v_codes_%d" % t)
-            v_scales[t] = tile([P, P], U8, "v_scales_%d" % t)
-            nc.vector.quantize_mx(v_codes[t][:].bitcast(FP8X4), v_scales[t][:], v[:])
+                nc.tensor.transpose(turned_pairs[:, u, :], pairs[:, u : I // 2 : 2], ident[:])
+            v_turned[t] = tile([P, P * PACK], BF16, "v_%d" % t)
+            nc.scalar.copy(
+                v_turned[t][:].bitcast(F32).rearrange("s (c u) -> s c u", u=2),
+                turned_pairs[:].rearrange("s u c -> s c u"),
+            )
 
-        pool_bf16 = tile([P, T], BF16, "pool_bf16", "th_pos")
+        pool_bf16 = tile([P, T], BF16, "pool_bf16", reuse="th_pos")
         for c0 in range(0, T, CAST_PIECE):
-            nc.scalar.activation(pool_bf16[:, c0 : c0 + CAST_PIECE], pools[0][:, c0 : c0 + CAST_PIECE], ACT.Copy)
-        picked = tile([P, I], BF16, "picked_0")
+            piece = slice(c0, c0 + CAST_PIECE)
+            nc.scalar.activation(pool_bf16[:, piece], pools[SCALAR_PLANE][:, piece], ACT.Copy)
+        picked = tile([P, I], BF16, "picked_0", reuse="m_neg_1")
         nc.scalar.activation(picked[:], pool_bf16[:].indirect(offsets[:]), ACT.Copy)
-        turn_values(0, picked)
-
-        for t in range(1, PACK):
-            picked = tile([P, I], BF16, "picked_%d" % t, {1: "ua_1", 2: "x_1"}.get(t))
+        turn_values(SCALAR_PLANE, picked, "turn_outer")
+        for t, reuse, tag in ((1, "ua_1", "turn_inner"), (2, "x_1", "turn_inner"), (LAST_PLANE, None, "turn_outer")):
+            picked = tile([P, I], BF16, "picked_%d" % t, reuse=reuse)
             nc.vector.tensor_copy(picked[:], pools[t][:].indirect(offsets[:]))
-            turn_values(t, picked)
+            turn_values(t, picked, tag)
 
-        w_both = tile([P, HALVES, P, PACK], BF16, "w_both", "vals_3")
+        code_bytes = P * 4
+        w_codes, w_scales = [], []
         for h in range(HALVES):
-            turned = bank([P, PACK, P], "a%d" % h)
+            tw = bank([P, PACK, P], "a%d" % h)
             for j, term in enumerate(terms[h]):
                 for r in range(PACK):
                     nc.tensor.matmul(
-                        turned[:, r, :], term[:, r, :], ident[:], is_transpose=True,
-                        start=(j == 0 and r == 0), stop=(j == 1 and r == PACK - 1),
+                        tw[:, r, :],
+                        term[:, r, :],
+                        ident[:],
+                        is_transpose=True,
+                        start=(j == 0 and r == 0),
+                        stop=(j == 1 and r == PACK - 1),
                     )
-            w = w_both[:, h]
+            w = late_tile([P, P, PACK], BF16, "w_%d" % h, (PACK + HALVES + 2 * h) * code_bytes)
             nc.vector.tensor_tensor(
-                w, turned[:].rearrange("s r q -> s q r"),
-                os_sb[:].unsqueeze(1).to_broadcast([P, P, PACK]), ALU.mult,
+                w[:],
+                tw[:].rearrange("s r q -> s q r"),
+                factor[:].unsqueeze(1).to_broadcast([P, P, PACK]),
+                ALU.mult,
             )
-            w_codes.append(tile([P, P], U32, "w_codes_%d" % h))
+            w_codes.append(late_tile([P, P], U32, "w_codes_%d" % h, (PACK + h) * code_bytes))
             w_scales.append(tile([P, P], U8, "w_scales_%d" % h))
-            nc.vector.quantize_mx(w_codes[h][:].bitcast(FP8X4), w_scales[h][:], w.rearrange("s q r -> s (q r)"))
+            nc.vector.quantize_mx(w_codes[h][:].bitcast(FP8X4), w_scales[h][:], w[:].rearrange("s q r -> s (q r)"))
 
-        out_rows = out_0.rearrange("(p t) (h q) -> h p t q", t=PACK, h=HALVES)
-        out_words = out_1[0].rearrange("p c t -> p (c t)").bitcast(I32)
+        early_planes = (1, 2, SCALAR_PLANE)
+        v_codes, v_scales = {}, {}
+        for t in early_planes + (LAST_PLANE,):
+            v_codes[t] = late_tile([P, P], U32, "v_codes_%d" % t, t * code_bytes)
+            v_scales[t] = tile([P, P], U8, "v_scales_%d" % t)
+            nc.vector.quantize_mx(v_codes[t][:].bitcast(FP8X4), v_scales[t][:], v_turned[t][:])
+
+        acc = [bank([P, PACK, P], "b%d" % h) for h in range(HALVES)]
+        for planes in (early_planes, (LAST_PLANE,)):
+            for h in range(HALVES):
+                for t in planes:
+                    nc.tensor.matmul_mx(
+                        acc[h][:, t, :],
+                        lhsT=v_codes[t][:].bitcast(FP8X4),
+                        lhsT_scale=v_scales[t][:],
+                        rhs=w_codes[h][:].bitcast(FP8X4),
+                        rhs_scale=w_scales[h][:],
+                        start=True,
+                        stop=True,
+                    )
+        o_grouped = tile([P, Q, PACK], BF16, "o_grouped")
+        result = tile([P, PACK, Q], F32, "result")
+        for h, copy in enumerate((nc.vector.tensor_copy, nc.scalar.copy)):
+            cols = slice(h * P, (h + 1) * P)
+            copy(result[:, :, cols], acc[h][:])
+            copy(o_grouped[:, cols, :], acc[h][:].rearrange("p t q -> p q t"))
+        nc.sync.dma_start(out_0.rearrange("(p t) q -> p t q", t=PACK), result[:])
         o_codes = tile([P, Q], U32, "o_codes")
         o_scales = tile([P, Q], U8, "o_scales")
-        for h, copy in enumerate((nc.scalar.copy, nc.vector.tensor_copy)):
-            cols = slice(h * P, (h + 1) * P)
-            acc = bank([P, PACK, P], "b%d" % h)
-            for t in range(PACK):
-                nc.tensor.matmul_mx(
-                    acc[:, t, :],
-                    lhsT=v_codes[t][:].bitcast(FP8X4), lhsT_scale=v_scales[t][:],
-                    rhs=w_codes[h][:].bitcast(FP8X4), rhs_scale=w_scales[h][:],
-                    start=True, stop=True,
-                )
-            o_grouped = tile([P, P, PACK], BF16, "o_grouped_%d" % h)
-            copy(o_grouped[:], acc[:].rearrange("p t q -> p q t"))
-            result = tile([P, PACK, P], F32, "result_%d" % h)
-            nc.scalar.copy(result[:], acc[:])
-            nc.scalar.dma_start(out_rows[h], result[:])
-            nc.vector.quantize_mx(
-                o_codes[:, cols].bitcast(FP8X4), o_scales[:, cols], o_grouped[:].rearrange("p q t -> p (q t)")
-            )
-            nc.sync.dma_start(out_words[:, cols], o_codes[:, cols].bitcast(I32))
-        for g in range(4):
-            nc.sync.dma_start(
+        nc.vector.quantize_mx(o_codes[:].bitcast(FP8X4), o_scales[:], o_grouped[:].rearrange("p q t -> p (q t)"))
+        nc.sync.dma_start(out_1[0].rearrange("p c t -> p (c t)").bitcast(I32), o_codes[:].bitcast(I32))
+        for g in range(P // QUADRANT):
+            queue = nc.sync if g % 2 == 0 else nc.scalar
+            queue.dma_start(
                 out_2[0, 4 * g : 4 * g + 4, :].bitcast(I32),
-                o_scales[32 * g : 32 * g + 4, :].bitcast(I32),
+                o_scales[QUADRANT * g : QUADRANT * g + 4, :].bitcast(I32),
             )

from contextlib import ExitStack

import concourse.mybir as mybir
from concourse.masks import make_identity

D, E, T, I, Q = 512, 512, 2048, 512, 256
P = 128
PACK = 4
HALVES = Q // P
QUADRANT = 32
RUN = 4
CAST_PIECE = 512
SCALAR_PLANE = 0
LAST_PLANE = PACK - 1
FLOPS = 2 * (3 * D * Q * I + I * E * Q)

F32 = mybir.dt.float32
BF16 = mybir.dt.bfloat16
I32 = mybir.dt.int32
U32 = mybir.dt.uint32
U16 = mybir.dt.uint16
U8 = mybir.dt.uint8
FP8X4 = mybir.dt.float8_e4m3fn_x4
FP4X4 = mybir.dt.float4_e2m1fn_x4
ALU = mybir.AluOpType
ACT = mybir.ActivationFunctionType


def tile_attend_tteitherquestion_pl_kernel(
    tc, query, dquery, query2, keys_words, keys_scales, th, slot_factor, vals, offs, out_0, out_1, out_2
):
    nc = tc.nc
    with ExitStack() as ctx:
        sb = ctx.enter_context(tc.tile_pool(name="sb", bufs=1))
        late = ctx.enter_context(tc.tile_pool(name="late", bufs=1))
        psum = ctx.enter_context(tc.psum_pool(name="psum", bufs=1))

        def tile(shape, dtype, name, reuse=None):
            return sb.tile(shape, dtype, name=name, tag=reuse or name, align_bytes=64)

        def late_tile(shape, dtype, name, offset):
            return late.tile(shape, dtype, name=name, align_bytes=64, offset=offset)

        def bank(shape, tag):
            return psum.tile(shape, F32, name=tag, tag=tag)

        offsets = sb.tile([P, I // 16], U16, name="offsets")
        nc.sync.dma_start(offsets[:], offs)
        key_scales = tile([P, T], U8, "key_scales")
        for g in range(P // QUADRANT):
            nc.sync.dma_start(
                key_scales[QUADRANT * g : QUADRANT * (g + 1), :].bitcast(I32),
                keys_scales[0, 4 * g : 4 * g + 4, :].bitcast(I32).partition_broadcast(QUADRANT // 4),
            )
        key_words = tile([P, T], U16, "key_words")
        nc.sync.dma_start(key_words[:].bitcast(I32), keys_words[0].bitcast(I32))
        raw = {}
        th_pos = tile([P, HALVES], F32, "th_pos")
        factor = tile([P, PACK], F32, "factor")
        for name, src in (("a", query), ("b", query2), ("ta", dquery)):
            raw[name] = tile([P, PACK, Q], F32, "raw_" + name)
            nc.sync.dma_start(raw[name][:], src.rearrange("(p t) q -> p t q", t=PACK))
        with nc.allow_non_contiguous_dma(reason="one threshold to a partition for each half of the rows"):
            nc.scalar.dma_start(th_pos[:], th.rearrange("(h p) o -> p (h o)", p=P))
        nc.scalar.dma_start(factor[:], slot_factor.rearrange("o (s r) -> (o s) r", r=PACK))
        val_planes = vals.rearrange("(p t) n -> t p n", t=PACK)
        pools = []
        for t in range(PACK):
            pools.append(late_tile([P, T], F32, "vals_last", 0) if t == LAST_PLANE else tile([P, T], F32, "vals_%d" % t))
            nc.sync.dma_start(pools[t][:], val_planes[t])

        ident = tile([P, P], F32, "ident")
        make_identity(nc, ident[:])
        warm = tile([P, 1], F32, "warm")
        nc.scalar.activation(warm[:], ident[:, 0:1], ACT.Sigmoid)
        th_neg = tile([P, HALVES], F32, "th_neg")
        nc.gpsimd.tensor_scalar(th_neg[:], th_pos[:], -1.0, 0.0, ALU.mult, ALU.add)

        picked_scales = tile([P, I], U8, "picked_scales")
        nc.vector.tensor_copy(picked_scales[:], key_scales[:].indirect(offsets[:]))
        picked_words = tile([P, I], U16, "picked_words")
        nc.vector.tensor_copy(picked_words[:], key_words[:].indirect(offsets[:]))

        scores = {}
        for name in ("a", "b", "ta"):
            grouped = []
            for h in range(HALVES):
                grouped.append(tile([P, P * PACK], BF16, "grouped_%s%d" % (name, h)))
                nc.vector.tensor_copy(
                    grouped[h][:].rearrange("p (c i t) -> p c t i", i=RUN, t=PACK),
                    raw[name][:, :, h * P : (h + 1) * P].rearrange("p t (c i) -> p c t i", i=RUN),
                )
            for h in range(HALVES):
                codes = tile([P, P], U32, "codes_%s%d" % (name, h))
                scales = tile([P, P], U8, "scales_%s%d" % (name, h))
                nc.vector.quantize_mx(codes[:].bitcast(FP8X4), scales[:], grouped[h][:])
                scores[name, h] = bank([P, I], "%s%d" % (name, h))
                nc.tensor.matmul_mx(
                    scores[name, h][:],
                    lhsT=codes[:].bitcast(FP8X4),
                    lhsT_scale=scales[:],
                    rhs=picked_words[:].bitcast(FP4X4),
                    rhs_scale=picked_scales[:],
                    start=True,
                    stop=True,
                )

        terms = []
        for h in range(HALVES):
            ua, nb, m_neg, p_neg, x, tp_term, p_term = [
                tile([P, I], F32, "%s_%d" % (name, h))
                for name in ("ua", "nb", "m_neg", "p_neg", "x", "tp_term", "p_term")
            ]
            sum_neg, r_neg, c, k = [tile([P, 1], F32, "%s_%d" % (name, h)) for name in ("sum_neg", "r_neg", "c", "k")]
            nc.scalar.activation(ua[:], scores["a", h][:], ACT.Sigmoid, bias=th_neg[:, h : h + 1])
            nc.scalar.activation(nb[:], scores["b", h][:], ACT.Sigmoid, bias=th_pos[:, h : h + 1], scale=-1.0)
            nc.vector.scalar_tensor_tensor(m_neg[:], ua[:], 1.0, nb[:], ALU.subtract, ALU.mult)
            nc.scalar.activation(p_neg[:], m_neg[:], ACT.Identity, bias=-1.0, scale=-1.0, accum_out=sum_neg[:])
            nc.vector.tensor_tensor(x[:], scores["ta", h][:], ua[:], ALU.mult)
            nc.vector.reciprocal(r_neg[:], sum_neg[:])
            nc.vector.scalar_tensor_tensor(tp_term[:], x[:], r_neg[:], m_neg[:], ALU.mult, ALU.mult, accum_out=c[:])
            nc.scalar.activation(k[:], c[:], ACT.Copy, scale=r_neg[:])
            nc.scalar.activation(
                p_term[:].rearrange("q (r s) -> q s r", r=PACK),
                m_neg[:].rearrange("q (s r) -> q s r", r=PACK),
                ACT.Identity,
                bias=k[:],
                scale=k[:],
            )
            terms.append(
                (tp_term[:].rearrange("q (s r) -> q r s", r=PACK), p_term[:].rearrange("q (r s) -> q r s", r=PACK))
            )

        v_turned = {}

        def turn_values(t, picked, tag):
            pairs = picked[:].bitcast(F32)
            turned_pairs = bank([P, 2, P], tag)
            for u in range(2):
                nc.tensor.transpose(turned_pairs[:, u, :], pairs[:, u : I // 2 : 2], ident[:])
            v_turned[t] = tile([P, P * PACK], BF16, "v_%d" % t)
            nc.scalar.copy(
                v_turned[t][:].bitcast(F32).rearrange("s (c u) -> s c u", u=2),
                turned_pairs[:].rearrange("s u c -> s c u"),
            )

        pool_bf16 = tile([P, T], BF16, "pool_bf16", reuse="th_pos")
        for c0 in range(0, T, CAST_PIECE):
            piece = slice(c0, c0 + CAST_PIECE)
            nc.scalar.activation(pool_bf16[:, piece], pools[SCALAR_PLANE][:, piece], ACT.Copy)
        picked = tile([P, I], BF16, "picked_0", reuse="m_neg_1")
        nc.scalar.activation(picked[:], pool_bf16[:].indirect(offsets[:]), ACT.Copy)
        turn_values(SCALAR_PLANE, picked, "turn_outer")
        for t, reuse, tag in ((1, "ua_1", "turn_inner"), (2, "x_1", "turn_inner"), (LAST_PLANE, None, "turn_outer")):
            picked = tile([P, I], BF16, "picked_%d" % t, reuse=reuse)
            nc.vector.tensor_copy(picked[:], pools[t][:].indirect(offsets[:]))
            turn_values(t, picked, tag)

        code_bytes = P * 4
        w_codes, w_scales = [], []
        for h in range(HALVES):
            tw = bank([P, PACK, P], "a%d" % h)
            for j, term in enumerate(terms[h]):
                for r in range(PACK):
                    nc.tensor.matmul(
                        tw[:, r, :],
                        term[:, r, :],
                        ident[:],
                        is_transpose=True,
                        start=(j == 0 and r == 0),
                        stop=(j == 1 and r == PACK - 1),
                    )
            w = late_tile([P, P, PACK], BF16, "w_%d" % h, (PACK + HALVES + 2 * h) * code_bytes)
            nc.vector.tensor_tensor(
                w[:],
                tw[:].rearrange("s r q -> s q r"),
                factor[:].unsqueeze(1).to_broadcast([P, P, PACK]),
                ALU.mult,
            )
            w_codes.append(late_tile([P, P], U32, "w_codes_%d" % h, (PACK + h) * code_bytes))
            w_scales.append(tile([P, P], U8, "w_scales_%d" % h))
            nc.vector.quantize_mx(w_codes[h][:].bitcast(FP8X4), w_scales[h][:], w[:].rearrange("s q r -> s (q r)"))

        early_planes = (1, 2, SCALAR_PLANE)
        v_codes, v_scales = {}, {}
        for t in early_planes + (LAST_PLANE,):
            v_codes[t] = late_tile([P, P], U32, "v_codes_%d" % t, t * code_bytes)
            v_scales[t] = tile([P, P], U8, "v_scales_%d" % t)
            nc.vector.quantize_mx(v_codes[t][:].bitcast(FP8X4), v_scales[t][:], v_turned[t][:])

        acc = [bank([P, PACK, P], "b%d" % h) for h in range(HALVES)]
        for planes in (early_planes, (LAST_PLANE,)):
            for h in range(HALVES):
                for t in planes:
                    nc.tensor.matmul_mx(
                        acc[h][:, t, :],
                        lhsT=v_codes[t][:].bitcast(FP8X4),
                        lhsT_scale=v_scales[t][:],
                        rhs=w_codes[h][:].bitcast(FP8X4),
                        rhs_scale=w_scales[h][:],
                        start=True,
                        stop=True,
                    )
        o_grouped = tile([P, Q, PACK], BF16, "o_grouped")
        result = tile([P, PACK, Q], F32, "result")
        for h, copy in enumerate((nc.vector.tensor_copy, nc.scalar.copy)):
            cols = slice(h * P, (h + 1) * P)
            copy(result[:, :, cols], acc[h][:])
            copy(o_grouped[:, cols, :], acc[h][:].rearrange("p t q -> p q t"))
        nc.sync.dma_start(out_0.rearrange("(p t) q -> p t q", t=PACK), result[:])
        o_codes = tile([P, Q], U32, "o_codes")
        o_scales = tile([P, Q], U8, "o_scales")
        nc.vector.quantize_mx(o_codes[:].bitcast(FP8X4), o_scales[:], o_grouped[:].rearrange("p q t -> p (q t)"))
        nc.sync.dma_start(out_1[0].rearrange("p c t -> p (c t)").bitcast(I32), o_codes[:].bitcast(I32))
        for g in range(P // QUADRANT):
            queue = nc.sync if g % 2 == 0 else nc.scalar
            queue.dma_start(
                out_2[0, 4 * g : 4 * g + 4, :].bitcast(I32),
                o_scales[QUADRANT * g : QUADRANT * g + 4, :].bitcast(I32),
            )
